import numpy as np
import ml_dtypes


def mxq(x, axis, fmt="e4m3"):
    dtype, down = {"e4m3": (ml_dtypes.float8_e4m3fn, 7), "e5m2": (ml_dtypes.float8_e5m2, 14)}[fmt]
    v = np.moveaxis(np.asarray(x, np.float32).astype(ml_dtypes.bfloat16).astype(np.float64), axis, -1)
    blocks = v.reshape(v.shape[:-1] + (-1, 32))
    amax = np.abs(blocks).max(-1, keepdims=True)
    byte = np.maximum(np.where(amax > 0, np.frexp(amax)[1] - 1 + 127, 0) - down, 1)
    scale = np.exp2(byte - 127.0)
    codes = (blocks / scale).astype(np.float32).astype(dtype).astype(np.float64)
    return np.moveaxis((codes * scale).reshape(v.shape), -1, axis)


WIDE = False


def mx_kscale(k):
    if not WIDE:
        return np.ones(k)
    levels = np.array([10, -10, 5, -5, 0])
    if k % 512:
        return np.exp2(np.random.permutation(np.resize(levels, k // 32))).repeat(32)
    a = np.empty((k // 512, 16))
    for p in range(k // 512):
        a[p, :8] = np.random.permutation(np.resize(levels, 8))
        for g in range(8):
            far = levels[np.abs(levels - a[p, g]) >= 10]
            a[p, g + 8] = far[np.random.randint(len(far))]
    return np.exp2(a.ravel()).repeat(32)


def f64(x):
    return np.asarray(x).astype(np.float64)


def striped(idx):
    return np.tile(idx.reshape(-1, 16).T, (8, 1)).astype(np.uint16)


def unstriped(offs):
    return offs[:16].T.reshape(-1).astype(np.int64)


def striped8(idx):
    return np.concatenate([x.reshape(-1, 16).T for x in idx]).astype(np.uint16)


def runs(offs, k):
    lists = np.stack([offs[16 * r : 16 * r + 16].T.reshape(-1) for r in range(8)]).astype(np.int64)
    return lists[np.arange(k) % 512 // 64]


def pack_weight(w):
    k, n = w.shape
    w = f64(np.asarray(w, np.float32).astype(ml_dtypes.bfloat16)).reshape(k // 32, 32, n)
    amax = np.abs(w).max(1)
    byte = np.clip(np.where(amax > 0, np.frexp(amax)[1] - 1 + 127 - 7, 1), 1, 254)
    scaled = (w * np.exp2(127.0 - byte)[:, None, :]).reshape(k, n).astype(np.float32)
    words = np.ascontiguousarray(scaled.reshape(k // 512, 128, 4, n).transpose(0, 1, 3, 2)).astype(ml_dtypes.float8_e4m3fn).view(np.uint8)
    return words, np.ascontiguousarray(byte.astype(np.uint8).reshape(k // 512, 16, n))


def unpack_weight(words, scales):
    g, p, n, _ = words.shape
    vals = np.ascontiguousarray(words).view(ml_dtypes.float8_e4m3fn).astype(np.float64) * np.repeat(np.exp2(scales.astype(np.float64) - 127.0), 8, axis=1)[..., None]
    return vals.transpose(0, 1, 3, 2).reshape(g * 512, n)


def sigmoid(v):
    return 1.0 / (1.0 + np.exp(-np.maximum(v, -700.0)))


K, T, S, N, H, J = 512, 2048, 256, 512, 512, 512


def setup_inputs():
    n = np.random.standard_normal
    s = mx_kscale(K)[:, None]
    u = mx_kscale(H)
    packed_xT = pack_weight(n((K, T)) * s)
    return {
        "x_words": packed_xT[0],
        "x_scales": packed_xT[1],
        "w1": (n((K, H)) / np.sqrt(K) / s).astype(np.float32),
        "gn": (np.random.uniform(0.5, 1.5, (H, 1)) * u[:, None]).astype(np.float32),
        "gm": (np.random.uniform(0.5, 1.5, (H, 1)) * u[:, None]).astype(np.float32),
        "w2": (n((H, N)) / np.sqrt(2 * H) / u[:, None]).astype(np.float32),
        "w3": (n((H, N)) / np.sqrt(2 * H) / u[:, None]).astype(np.float32),
        "offs": striped(np.random.permutation(T)[:S]),
        "n1": striped(np.random.randint(0, S, J)),
        "n2": striped8(np.stack([np.random.permutation(S) for _ in range(8)])),
        "n3": striped8(np.stack([np.random.permutation(S) for _ in range(8)])),
        "n4": striped8(np.stack([np.random.permutation(S) for _ in range(8)])),
        "n5": striped8(np.stack([np.random.permutation(S) for _ in range(8)])),
    }


def reference(x_words, x_scales, w1, gn, gm, w2, w3, offs, n1, n2, n3, n4, n5):
    xq = unpack_weight(x_words, x_scales)[:, unstriped(offs)]
    y = mxq(f64(w1), 0, "e4m3").T @ xq
    mb = y[:, unstriped(n1)]
    ms = mb.reshape(H, S, 2).sum(axis=2)
    mx = mb.reshape(H, S, 2).max(axis=2)
    z = f64(gn) * (ms - np.maximum(y, mx))
    z2 = f64(gm) * (y + y[np.arange(H)[:, None], runs(n2, H)] - (np.maximum(y[np.arange(H)[:, None], runs(n3, H)], y[np.arange(H)[:, None], runs(n4, H)])))
    h = mxq(f64(w2), 0, "e4m3").T @ mxq(z, 0, "e4m3") + mxq(f64(w3), 0, "e4m3").T @ mxq(z2, 0, "e4m3")
    return h * (sigmoid(h[np.arange(N)[:, None], runs(n5, N)]))

@@ -1,0 +1,208 @@
+from contextlib import ExitStack
+
+import concourse.mybir as mybir
+
+K, T, S, N, H, J = 512, 2048, 256, 512, 512, 512
+FLOPS = 2 * S * (K * H + 2 * H * N)
+
+F32 = mybir.dt.float32
+BF16 = mybir.dt.bfloat16
+I32 = mybir.dt.int32
+U32 = mybir.dt.uint32
+U16 = mybir.dt.uint16
+U8 = mybir.dt.uint8
+FP8X4 = mybir.dt.float8_e4m3fn_x4
+ALU = mybir.AluOpType
+ACT = mybir.ActivationFunctionType
+
+P = 128
+PACK = 4
+HALF = S // 2
+Y_WINDOW = 1024
+H_WINDOW = 512
+
+
+def tile_picked_joingpairtrimgate_none_p_kernel(
+    tc, x_words, x_scales, w1, gn, gm, w2, w3, offs, n1, n2, n3, n4, n5, out
+):
+    nc = tc.nc
+    with ExitStack() as ctx:
+        sb = ctx.enter_context(tc.tile_pool(name="sb", bufs=1))
+        ps = ctx.enter_context(tc.psum_pool(name="ps", bufs=1))
+
+        def tile(name, shape, dtype):
+            return sb.tile(shape, dtype, name=name, align_bytes=64)
+
+        def load_list(name, src):
+            lst = tile(name, list(src.shape), U16)
+            nc.sync.dma_start(lst[:], src)
+            return lst
+
+        def load_weight(name, src):
+            raw = tile(name, [P, PACK, src.shape[1]], F32)
+            nc.sync.dma_start(raw[:], src.rearrange("(p j) c -> p j c", j=PACK))
+            return raw
+
+        def quantize(name, grouped, width):
+            codes = tile(name + "_codes", [P, width], U32)
+            scales = tile(name + "_scales", [P, width], U8)
+            nc.vector.quantize_mx(out=codes[:].bitcast(FP8X4), scales=scales[:], in_=grouped[:])
+            return codes, scales
+
+        def mx(dst, lhs, lhs_cols, rhs, rhs_cols, start, stop):
+            nc.tensor.matmul_mx(
+                out=dst,
+                lhsT=lhs[0][:, lhs_cols].bitcast(FP8X4),
+                lhsT_scale=lhs[1][:, lhs_cols],
+                rhs=rhs[0][:, rhs_cols].bitcast(FP8X4),
+                rhs_scale=rhs[1][:, rhs_cols],
+                start=start,
+                stop=stop,
+            )
+
+        scale_table = tile("scale_table", [P, T], U8)
+        nc.vector.memset(scale_table[:].bitcast(I32), 0)
+        offs_sb = load_list("offs_sb", offs)
+        w1_raw = load_weight("w1_raw", w1)
+        for quad in range(4):
+            nc.scalar.dma_start(
+                scale_table[32 * quad : 32 * quad + 4, :].bitcast(I32),
+                x_scales[0, 4 * quad : 4 * quad + 4, :].bitcast(I32),
+            )
+        word_table = tile("word_table", [P, T], U32)
+        nc.sync.dma_start(word_table[:].bitcast(I32), x_words[0].rearrange("p n t -> p (n t)").bitcast(I32))
+        n1_sb = load_list("n1_sb", n1)
+        n3_sb = load_list("n3_sb", n3)
+        n4_sb = load_list("n4_sb", n4)
+        gn_sb = tile("gn_sb", [P, PACK], F32)
+        gm_sb = tile("gm_sb", [P, PACK], F32)
+        nc.sync.dma_start(gm_sb[:], gm.rearrange("(p t) o -> p (t o)", t=PACK))
+        w2_raw = load_weight("w2_raw", w2)
+        n2_sb = load_list("n2_sb", n2)
+        n5_sb = load_list("n5_sb", n5)
+        w3_raw = load_weight("w3_raw", w3)
+        nc.sync.dma_start(gn_sb[:], gn.rearrange("(p t) o -> p (t o)", t=PACK))
+
+        x_sc = tile("x_sc", [P, S], U8)
+        nc.vector.tensor_copy(x_sc[:], scale_table[:].indirect(offs_sb[:]))
+
+        w1_q = []
+        w1_view = w1_raw[:].rearrange("p j (m t) -> p m j t", t=PACK)
+        w1_grouped = [tile("w1_grouped%d" % u, [P, 2 * P * PACK], BF16) for u in range(2)]
+        dsts = [g[:].rearrange("p (t m j) -> p m j t", t=2, j=PACK) for g in w1_grouped]
+        nc.vector.tensor_copy(dsts[0], w1_view[:, :, :, 0:2])
+        nc.scalar.activation(dsts[1], w1_view[:, :, :, 2:4], ACT.Copy)
+        for u in range(2):
+            w1_q.append(quantize("w1_%d" % u, w1_grouped[u], 2 * P))
+
+        x_cd = tile("x_cd", [P, S], U32)
+        nc.vector.tensor_copy(x_cd[:], word_table[:].bitcast(U32).indirect(offs_sb[:]))
+        x_q = (x_cd, x_sc)
+
+        y_ps = [ps.tile([P, S], F32, name="y_ps%d" % t, tag="late%d" % t) for t in range(PACK)]
+        for t in range(PACK):
+            mx(y_ps[t][:], w1_q[t // 2], slice(P * (t % 2), P * (t % 2 + 1)), x_q, slice(0, S), True, True)
+
+        y_win = [tile("y_win%d" % t, [P, Y_WINDOW], F32) for t in range(PACK)]
+        nc.scalar.activation(y_win[0][:, 0:S], y_ps[0][:], ACT.Copy)
+        for t in range(1, PACK):
+            nc.vector.tensor_copy(y_win[t][:, 0:S], y_ps[t][:])
+
+        members = [tile("members%d" % t, [P, J], F32) for t in range(PACK)]
+        for t in range(PACK):
+            nc.scalar.activation(members[t][:], y_win[t][:].indirect(n1_sb[:]), ACT.Copy)
+        at_n3 = [tile("at_n3_%d" % t, [P, S], F32) for t in range(PACK)]
+        at_n4 = [tile("at_n4_%d" % t, [P, S], F32) for t in range(PACK)]
+        for t in range(PACK):
+            nc.scalar.activation(at_n3[t][:], y_win[t][:].indirect(n3_sb[:]), ACT.Copy)
+            nc.scalar.activation(at_n4[t][:], y_win[t][:].indirect(n4_sb[:]), ACT.Copy)
+
+        yg_win = [tile("yg_win%d" % t, [P, S], F32) for t in range(PACK)]
+        for t in range(PACK):
+            nc.vector.tensor_scalar(yg_win[t][:], y_win[t][:, 0:S], gm_sb[:, t : t + 1], None, ALU.mult)
+
+        at_n2 = [tile("at_n2_%d" % h, [P, PACK, HALF], F32) for h in range(2)]
+        for h in range(2):
+            for t in range(PACK):
+                nc.scalar.activation(at_n2[h][:, t, :], yg_win[t][:].indirect(n2_sb[:, 8 * h : 8 * h + 8]), ACT.Copy)
+
+        def round_weight(name, raw, t):
+            grouped = tile("%s_grouped%d" % (name, t), [P, P * PACK], BF16)
+            nc.vector.tensor_copy(
+                grouped[:].rearrange("p (b q j) -> p b j q", q=4, j=PACK),
+                raw[:].rearrange("p j (b t q) -> p t b j q", t=PACK, q=4)[:, t],
+            )
+            return grouped
+
+        def weave(ap):
+            return ap.rearrange("p t (c i) -> p c t i", i=4)
+
+        trimmed = tile("trimmed", [P, PACK, S], F32)
+        w2_q = []
+        for t in range(PACK):
+            first = members[t][:, 0:J:2]
+            second = members[t][:, 1:J:2]
+            diff = tile("diff%d" % t, [P, S], F32)
+            part = tile("part%d" % t, [P, S], F32)
+            nc.vector.tensor_tensor(diff[:], second, y_ps[t][:], ALU.subtract)
+            grouped = round_weight("w2", w2_raw, t)
+            nc.vector.scalar_tensor_tensor(part[:], diff[:], 0.0, first, ALU.min, ALU.add)
+            w2_q.append(quantize("w2_%d" % t, grouped, P))
+            nc.vector.tensor_tensor(trimmed[:, t, :], part[:], second, ALU.min)
+
+        z_grouped = tile("z_grouped", [P, S * PACK], BF16)
+        nc.vector.tensor_tensor(
+            z_grouped[:].rearrange("p (c i t) -> p c t i", i=4, t=PACK),
+            weave(trimmed[:]),
+            gn_sb[:].unsqueeze(1).unsqueeze(3).to_broadcast([P, S // 4, PACK, 4]),
+            ALU.mult,
+        )
+
+        rest = tile("rest", [P, PACK, S], F32)
+        w3_q = []
+        z_q = None
+        for t in range(PACK):
+            larger = tile("larger%d" % t, [P, S], F32)
+            nc.vector.tensor_tensor(larger[:], at_n3[t][:], at_n4[t][:], ALU.max)
+            if t == 0:
+                z_q = quantize("z", z_grouped, S)
+            grouped = round_weight("w3", w3_raw, t)
+            nc.vector.scalar_tensor_tensor(
+                rest[:, t, :], larger[:], gm_sb[:, t : t + 1], yg_win[t][:], ALU.mult, ALU.subtract
+            )
+            w3_q.append(quantize("w3_%d" % t, grouped, P))
+
+        h_ps = [
+            [ps.tile([P, HALF], F32, name="h_ps%d_%d" % (h, t), tag=("early%d", "late%d")[h] % t) for t in range(PACK)]
+            for h in range(2)
+        ]
+        everything = slice(0, P)
+        for h in range(2):
+            for t in range(PACK):
+                mx(h_ps[h][t][:], w2_q[t], everything, z_q, slice(HALF * h, HALF * (h + 1)), True, False)
+
+        z2_grouped = [tile("z2_grouped%d" % h, [P, HALF * PACK], BF16) for h in range(2)]
+        for h in range(2):
+            nc.vector.tensor_tensor(
+                z2_grouped[h][:].rearrange("p (c i t) -> p c t i", i=4, t=PACK),
+                weave(at_n2[h][:]),
+                weave(rest[:, :, HALF * h : HALF * (h + 1)]),
+                ALU.subtract,
+            )
+        h_win = [tile("h_win%d" % t, [P, H_WINDOW], F32) for t in range(PACK)]
+        for h in range(2):
+            z2_q = quantize("z2_%d" % h, z2_grouped[h], HALF)
+            for t in range(PACK):
+                mx(h_ps[h][t][:], w3_q[t], everything, z2_q, everything, False, True)
+        for t in range(PACK):
+            nc.scalar.activation(h_win[t][:, 0:HALF], h_ps[0][t][:], ACT.Copy)
+        for t in range(PACK):
+            nc.vector.tensor_copy(h_win[t][:, HALF:S], h_ps[1][t][:])
+
+        out_view = out.rearrange("(b t q) s -> t b q s", t=PACK, q=4)
+        for t in range(PACK):
+            gate = tile("gate%d" % t, [P, S], F32)
+            nc.scalar.activation(gate[:], h_win[t][:].indirect(n5_sb[:]), ACT.Sigmoid)
+            res = tile("res%d" % t, [P, S], F32)
+            nc.vector.tensor_tensor(res[:], h_win[t][:, 0:S], gate[:], ALU.mult)
+            nc.sync.dma_start(out_view[t], res[:])

@@ -62,6 +62,9 @@ def tile_picked_joingpairtrimgate_none_p_kernel(
 
         scale_table = tile("scale_table", [P, T], U8)
         nc.vector.memset(scale_table[:].bitcast(I32), 0)
+        warm = tile("warm", [P, 2], F32)
+        nc.gpsimd.memset(warm[:, 0:1], 0.0)
+        nc.scalar.activation(warm[:, 1:2], warm[:, 0:1], ACT.Sigmoid)
         offs_sb = load_list("offs_sb", offs)
         w1_raw = load_weight("w1_raw", w1)
         for quad in range(4):
@@ -77,10 +80,10 @@ def tile_picked_joingpairtrimgate_none_p_kernel(
         gn_sb = tile("gn_sb", [P, PACK], F32)
         gm_sb = tile("gm_sb", [P, PACK], F32)
         nc.sync.dma_start(gm_sb[:], gm.rearrange("(p t) o -> p (t o)", t=PACK))
-        w2_raw = load_weight("w2_raw", w2)
+        w2_raw = [load_weight("w2_raw%d" % u, w2[:, u * N // 2 : (u + 1) * N // 2]) for u in range(2)]
         n2_sb = load_list("n2_sb", n2)
         n5_sb = load_list("n5_sb", n5)
-        w3_raw = load_weight("w3_raw", w3)
+        w3_raw = [load_weight("w3_raw%d" % u, w3[:, u * N // 2 : (u + 1) * N // 2]) for u in range(2)]
         nc.sync.dma_start(gn_sb[:], gn.rearrange("(p t) o -> p (t o)", t=PACK))
 
         x_sc = tile("x_sc", [P, S], U8)
@@ -103,13 +106,34 @@ def tile_picked_joingpairtrimgate_none_p_kernel(
         for t in range(PACK):
             mx(y_ps[t][:], w1_q[t // 2], slice(P * (t % 2), P * (t % 2 + 1)), x_q, slice(0, S), True, True)
 
-        y_win = [tile("y_win%d" % t, [P, Y_WINDOW], F32) for t in range(PACK)]
-        nc.scalar.activation(y_win[0][:, 0:S], y_ps[0][:], ACT.Copy)
-        for t in range(1, PACK):
-            nc.vector.tensor_copy(y_win[t][:, 0:S], y_ps[t][:])
+        def round_weight(grouped, raw, u):
+            nc.vector.tensor_copy(
+                grouped[:].rearrange("p (t u b q j) -> p u t b j q", t=PACK, u=2, q=4, j=PACK)[:, u],
+                raw[u][:].rearrange("p j (b t q) -> p t b j q", t=PACK, q=4),
+            )
 
+        def quantize_pair(grouped, q, pair):
+            cols = slice(2 * P * pair, 2 * P * (pair + 1))
+            nc.vector.quantize_mx(
+                out=q[0][:, cols].bitcast(FP8X4),
+                scales=q[1][:, cols],
+                in_=grouped[:, 2 * P * PACK * pair : 2 * P * PACK * (pair + 1)],
+            )
+
+        def weave(ap):
+            return ap.rearrange("p t (c i) -> p c t i", i=4)
+
+        w2_grouped = tile("w2_grouped", [P, N * PACK], BF16)
+        w3_grouped = tile("w3_grouped", [P, N * PACK], BF16)
+        w2_q = (tile("w2_codes", [P, N], U32), tile("w2_scales", [P, N], U8))
+        w3_q = (tile("w3_codes", [P, N], U32), tile("w3_scales", [P, N], U8))
+        round_weight(w2_grouped, w2_raw, 0)
+        round_weight(w2_grouped, w2_raw, 1)
+
+        y_win = [tile("y_win%d" % t, [P, Y_WINDOW], F32) for t in range(PACK)]
         members = [tile("members%d" % t, [P, J], F32) for t in range(PACK)]
         for t in range(PACK):
+            nc.scalar.activation(y_win[t][:, 0:S], y_ps[t][:], ACT.Copy)
             nc.scalar.activation(members[t][:], y_win[t][:].indirect(n1_sb[:]), ACT.Copy)
         at_n3 = [tile("at_n3_%d" % t, [P, S], F32) for t in range(PACK)]
         at_n4 = [tile("at_n4_%d" % t, [P, S], F32) for t in range(PACK)]
@@ -118,38 +142,39 @@ def tile_picked_joingpairtrimgate_none_p_kernel(
             nc.scalar.activation(at_n4[t][:], y_win[t][:].indirect(n4_sb[:]), ACT.Copy)
 
         yg_win = [tile("yg_win%d" % t, [P, S], F32) for t in range(PACK)]
-        for t in range(PACK):
+
+        def gain_y(t):
             nc.vector.tensor_scalar(yg_win[t][:], y_win[t][:, 0:S], gm_sb[:, t : t + 1], None, ALU.mult)
+
+        fillers = [
+            lambda: quantize_pair(w2_grouped, w2_q, 0),
+            lambda: quantize_pair(w2_grouped, w2_q, 1),
+            lambda: gain_y(0),
+            lambda: gain_y(1),
+            lambda: round_weight(w3_grouped, w3_raw, 0),
+            lambda: gain_y(2),
+            lambda: round_weight(w3_grouped, w3_raw, 1),
+            lambda: gain_y(3),
+        ]
+
+        trimmed = tile("trimmed", [P, PACK, S], F32)
+        scratch = [tile("scratch%d" % u, [P, S], F32) for u in range(2)]
+        for t in range(PACK):
+            first = members[t][:, 0:J:2]
+            second = members[t][:, 1:J:2]
+            diff, part = scratch[t % 2], scratch[1 - t % 2]
+            nc.vector.tensor_tensor(diff[:], second, y_ps[t][:], ALU.subtract)
+            fillers[2 * t]()
+            nc.vector.scalar_tensor_tensor(part[:], diff[:], 0.0, first, ALU.min, ALU.add)
+            fillers[2 * t + 1]()
+            nc.vector.tensor_tensor(trimmed[:, t, :], part[:], second, ALU.min)
 
         at_n2 = [tile("at_n2_%d" % h, [P, PACK, HALF], F32) for h in range(2)]
         for h in range(2):
             for t in range(PACK):
                 nc.scalar.activation(at_n2[h][:, t, :], yg_win[t][:].indirect(n2_sb[:, 8 * h : 8 * h + 8]), ACT.Copy)
 
-        def round_weight(name, raw, t):
-            grouped = tile("%s_grouped%d" % (name, t), [P, P * PACK], BF16)
-            nc.vector.tensor_copy(
-                grouped[:].rearrange("p (b q j) -> p b j q", q=4, j=PACK),
-                raw[:].rearrange("p j (b t q) -> p t b j q", t=PACK, q=4)[:, t],
-            )
-            return grouped
-
-        def weave(ap):
-            return ap.rearrange("p t (c i) -> p c t i", i=4)
-
-        trimmed = tile("trimmed", [P, PACK, S], F32)
-        w2_q = []
-        for t in range(PACK):
-            first = members[t][:, 0:J:2]
-            second = members[t][:, 1:J:2]
-            diff = tile("diff%d" % t, [P, S], F32)
-            part = tile("part%d" % t, [P, S], F32)
-            nc.vector.tensor_tensor(diff[:], second, y_ps[t][:], ALU.subtract)
-            grouped = round_weight("w2", w2_raw, t)
-            nc.vector.scalar_tensor_tensor(part[:], diff[:], 0.0, first, ALU.min, ALU.add)
-            w2_q.append(quantize("w2_%d" % t, grouped, P))
-            nc.vector.tensor_tensor(trimmed[:, t, :], part[:], second, ALU.min)
-
+        quantize_pair(w3_grouped, w3_q, 0)
         z_grouped = tile("z_grouped", [P, S * PACK], BF16)
         nc.vector.tensor_tensor(
             z_grouped[:].rearrange("p (c i t) -> p c t i", i=4, t=PACK),
@@ -157,20 +182,18 @@ def tile_picked_joingpairtrimgate_none_p_kernel(
             gn_sb[:].unsqueeze(1).unsqueeze(3).to_broadcast([P, S // 4, PACK, 4]),
             ALU.mult,
         )
+        quantize_pair(w3_grouped, w3_q, 1)
+        z_q = quantize("z", z_grouped, S)
 
         rest = tile("rest", [P, PACK, S], F32)
-        w3_q = []
-        z_q = None
-        for t in range(PACK):
-            larger = tile("larger%d" % t, [P, S], F32)
-            nc.vector.tensor_tensor(larger[:], at_n3[t][:], at_n4[t][:], ALU.max)
-            if t == 0:
-                z_q = quantize("z", z_grouped, S)
-            grouped = round_weight("w3", w3_raw, t)
-            nc.vector.scalar_tensor_tensor(
-                rest[:, t, :], larger[:], gm_sb[:, t : t + 1], yg_win[t][:], ALU.mult, ALU.subtract
-            )
-            w3_q.append(quantize("w3_%d" % t, grouped, P))
+        for step in range(PACK + 1):
+            if step < PACK:
+                nc.vector.tensor_tensor(trimmed[:, step, :], at_n3[step][:], at_n4[step][:], ALU.max)
+            if step > 0:
+                t = step - 1
+                nc.vector.scalar_tensor_tensor(
+                    rest[:, t, :], trimmed[:, t, :], gm_sb[:, t : t + 1], yg_win[t][:], ALU.mult, ALU.subtract
+                )
 
         h_ps = [
             [ps.tile([P, HALF], F32, name="h_ps%d_%d" % (h, t), tag=("early%d", "late%d")[h] % t) for t in range(PACK)]
@@ -179,21 +202,20 @@ def tile_picked_joingpairtrimgate_none_p_kernel(
         everything = slice(0, P)
         for h in range(2):
             for t in range(PACK):
-                mx(h_ps[h][t][:], w2_q[t], everything, z_q, slice(HALF * h, HALF * (h + 1)), True, False)
+                mx(h_ps[h][t][:], w2_q, slice(P * t, P * (t + 1)), z_q, slice(HALF * h, HALF * (h + 1)), True, False)
 
-        z2_grouped = [tile("z2_grouped%d" % h, [P, HALF * PACK], BF16) for h in range(2)]
+        z2_grouped = tile("z2_grouped", [P, HALF * PACK], BF16)
+        h_win = [tile("h_win%d" % t, [P, H_WINDOW], F32) for t in range(PACK)]
         for h in range(2):
             nc.vector.tensor_tensor(
-                z2_grouped[h][:].rearrange("p (c i t) -> p c t i", i=4, t=PACK),
+                z2_grouped[:].rearrange("p (c i t) -> p c t i", i=4, t=PACK),
                 weave(at_n2[h][:]),
                 weave(rest[:, :, HALF * h : HALF * (h + 1)]),
                 ALU.subtract,
             )
-        h_win = [tile("h_win%d" % t, [P, H_WINDOW], F32) for t in range(PACK)]
-        for h in range(2):
-            z2_q = quantize("z2_%d" % h, z2_grouped[h], HALF)
+            z2_q = quantize("z2_%d" % h, z2_grouped, HALF)
             for t in range(PACK):
-                mx(h_ps[h][t][:], w3_q[t], everything, z2_q, everything, False, True)
+                mx(h_ps[h][t][:], w3_q, slice(P * t, P * (t + 1)), z2_q, everything, False, True)
         for t in range(PACK):
             nc.scalar.activation(h_win[t][:, 0:HALF], h_ps[0][t][:], ACT.Copy)
         for t in range(PACK):

@@ -20,6 +20,7 @@ PACK = 4
 HALF = S // 2
 Y_WINDOW = 1024
 H_WINDOW = 512
+SCALAR_Y = (0,)
 
 
 def tile_picked_joingpairtrimgate_none_p_kernel(
@@ -61,14 +62,14 @@ def tile_picked_joingpairtrimgate_none_p_kernel(
             )
 
         scale_table = tile("scale_table", [P, T], U8)
-        nc.vector.memset(scale_table[:].bitcast(I32), 0)
+        nc.gpsimd.memset(scale_table[:].bitcast(I32), 0)
         warm = tile("warm", [P, 2], F32)
-        nc.gpsimd.memset(warm[:, 0:1], 0.0)
+        nc.vector.memset(warm[:, 0:1], 0.0)
         nc.scalar.activation(warm[:, 1:2], warm[:, 0:1], ACT.Sigmoid)
-        offs_sb = load_list("offs_sb", offs)
         w1_raw = load_weight("w1_raw", w1)
+        offs_sb = load_list("offs_sb", offs)
         for quad in range(4):
-            nc.scalar.dma_start(
+            nc.sync.dma_start(
                 scale_table[32 * quad : 32 * quad + 4, :].bitcast(I32),
                 x_scales[0, 4 * quad : 4 * quad + 4, :].bitcast(I32),
             )
@@ -80,21 +81,22 @@ def tile_picked_joingpairtrimgate_none_p_kernel(
         gn_sb = tile("gn_sb", [P, PACK], F32)
         gm_sb = tile("gm_sb", [P, PACK], F32)
         nc.sync.dma_start(gm_sb[:], gm.rearrange("(p t) o -> p (t o)", t=PACK))
-        w2_raw = [load_weight("w2_raw%d" % u, w2[:, u * N // 2 : (u + 1) * N // 2]) for u in range(2)]
+        w2_raw = [load_weight("w2_raw%d" % u, w2[:, u * N // 2 : (u + 1) * N // 2])[:] for u in range(2)]
         n2_sb = load_list("n2_sb", n2)
         n5_sb = load_list("n5_sb", n5)
-        w3_raw = [load_weight("w3_raw%d" % u, w3[:, u * N // 2 : (u + 1) * N // 2]) for u in range(2)]
+        w3_whole = load_weight("w3_raw", w3)
+        w3_raw = [w3_whole[:, :, u * N // 2 : (u + 1) * N // 2] for u in range(2)]
         nc.sync.dma_start(gn_sb[:], gn.rearrange("(p t) o -> p (t o)", t=PACK))
 
         x_sc = tile("x_sc", [P, S], U8)
         nc.vector.tensor_copy(x_sc[:], scale_table[:].indirect(offs_sb[:]))
 
         w1_q = []
-        w1_view = w1_raw[:].rearrange("p j (m t) -> p m j t", t=PACK)
+        w1_view = w1_raw[:].rearrange("p j (m t) -> p m t j", t=PACK)
         w1_grouped = [tile("w1_grouped%d" % u, [P, 2 * P * PACK], BF16) for u in range(2)]
-        dsts = [g[:].rearrange("p (t m j) -> p m j t", t=2, j=PACK) for g in w1_grouped]
-        nc.vector.tensor_copy(dsts[0], w1_view[:, :, :, 0:2])
-        nc.scalar.activation(dsts[1], w1_view[:, :, :, 2:4], ACT.Copy)
+        dsts = [g[:].rearrange("p (t m j) -> p m t j", t=2, j=PACK) for g in w1_grouped]
+        nc.vector.tensor_copy(dsts[0], w1_view[:, :, 0:2, :])
+        nc.scalar.activation(dsts[1], w1_view[:, :, 2:4, :], ACT.Copy)
         for u in range(2):
             w1_q.append(quantize("w1_%d" % u, w1_grouped[u], 2 * P))
 
@@ -102,129 +104,120 @@ def tile_picked_joingpairtrimgate_none_p_kernel(
         nc.vector.tensor_copy(x_cd[:], word_table[:].bitcast(U32).indirect(offs_sb[:]))
         x_q = (x_cd, x_sc)
 
-        y_ps = [ps.tile([P, S], F32, name="y_ps%d" % t, tag="late%d" % t) for t in range(PACK)]
+        y_ps = [ps.tile([P, S], F32, name="y_ps%d" % t) for t in range(PACK)]
         for t in range(PACK):
             mx(y_ps[t][:], w1_q[t // 2], slice(P * (t % 2), P * (t % 2 + 1)), x_q, slice(0, S), True, True)
 
         def round_weight(grouped, raw, u):
             nc.vector.tensor_copy(
                 grouped[:].rearrange("p (t u b q j) -> p u t b j q", t=PACK, u=2, q=4, j=PACK)[:, u],
-                raw[u][:].rearrange("p j (b t q) -> p t b j q", t=PACK, q=4),
+                raw[u].rearrange("p j (b t q) -> p t b j q", t=PACK, q=4),
             )
 
-        def quantize_pair(grouped, q, pair):
-            cols = slice(2 * P * pair, 2 * P * (pair + 1))
-            nc.vector.quantize_mx(
-                out=q[0][:, cols].bitcast(FP8X4),
-                scales=q[1][:, cols],
-                in_=grouped[:, 2 * P * PACK * pair : 2 * P * PACK * (pair + 1)],
-            )
+        def woven(grouped):
+            return grouped[:].rearrange("p (c i t) -> p c t i", i=4, t=PACK)
 
-        def weave(ap):
-            return ap.rearrange("p t (c i) -> p c t i", i=4)
+        def by_fours(planes):
+            return planes.rearrange("p t (c i) -> p c t i", i=4)
 
         w2_grouped = tile("w2_grouped", [P, N * PACK], BF16)
         w3_grouped = tile("w3_grouped", [P, N * PACK], BF16)
-        w2_q = (tile("w2_codes", [P, N], U32), tile("w2_scales", [P, N], U8))
-        w3_q = (tile("w3_codes", [P, N], U32), tile("w3_scales", [P, N], U8))
         round_weight(w2_grouped, w2_raw, 0)
-        round_weight(w2_grouped, w2_raw, 1)
 
         y_win = [tile("y_win%d" % t, [P, Y_WINDOW], F32) for t in range(PACK)]
-        members = [tile("members%d" % t, [P, J], F32) for t in range(PACK)]
+        members = [tile("members%d" % u, [P, 2, J], F32) for u in range(2)]
         for t in range(PACK):
-            nc.scalar.activation(y_win[t][:, 0:S], y_ps[t][:], ACT.Copy)
-            nc.scalar.activation(members[t][:], y_win[t][:].indirect(n1_sb[:]), ACT.Copy)
-        at_n3 = [tile("at_n3_%d" % t, [P, S], F32) for t in range(PACK)]
-        at_n4 = [tile("at_n4_%d" % t, [P, S], F32) for t in range(PACK)]
-        for t in range(PACK):
-            nc.scalar.activation(at_n3[t][:], y_win[t][:].indirect(n3_sb[:]), ACT.Copy)
-            nc.scalar.activation(at_n4[t][:], y_win[t][:].indirect(n4_sb[:]), ACT.Copy)
-
+            if t in SCALAR_Y:
+                nc.scalar.activation(y_win[t][:, 0:S], y_ps[t][:], ACT.Copy)
+            else:
+                nc.vector.tensor_copy(y_win[t][:, 0:S], y_ps[t][:])
+            nc.scalar.activation(members[t // 2][:, t % 2, :], y_win[t][:].indirect(n1_sb[:]), ACT.Copy)
         yg_win = [tile("yg_win%d" % t, [P, S], F32) for t in range(PACK)]
+        at_n3 = [tile("at_n3_%d" % u, [P, 2, S], F32) for u in range(2)]
+        at_n4 = [tile("at_n4_%d" % u, [P, 2, S], F32) for u in range(2)]
+        for t in range(PACK):
+            nc.scalar.activation(at_n3[t // 2][:, t % 2, :], y_win[t][:].indirect(n3_sb[:]), ACT.Copy)
+            nc.scalar.activation(at_n4[t // 2][:, t % 2, :], y_win[t][:].indirect(n4_sb[:]), ACT.Copy)
+            nc.scalar.activation(yg_win[t][:], y_win[t][:, 0:S], ACT.Copy, scale=gm_sb[:, t : t + 1])
 
-        def gain_y(t):
-            nc.vector.tensor_scalar(yg_win[t][:], y_win[t][:, 0:S], gm_sb[:, t : t + 1], None, ALU.mult)
-
-        fillers = [
-            lambda: quantize_pair(w2_grouped, w2_q, 0),
-            lambda: quantize_pair(w2_grouped, w2_q, 1),
-            lambda: gain_y(0),
-            lambda: gain_y(1),
-            lambda: round_weight(w3_grouped, w3_raw, 0),
-            lambda: gain_y(2),
-            lambda: round_weight(w3_grouped, w3_raw, 1),
-            lambda: gain_y(3),
-        ]
+        round_weight(w2_grouped, w2_raw, 1)
 
         trimmed = tile("trimmed", [P, PACK, S], F32)
-        scratch = [tile("scratch%d" % u, [P, S], F32) for u in range(2)]
-        for t in range(PACK):
-            first = members[t][:, 0:J:2]
-            second = members[t][:, 1:J:2]
-            diff, part = scratch[t % 2], scratch[1 - t % 2]
-            nc.vector.tensor_tensor(diff[:], second, y_ps[t][:], ALU.subtract)
-            fillers[2 * t]()
-            nc.vector.scalar_tensor_tensor(part[:], diff[:], 0.0, first, ALU.min, ALU.add)
-            fillers[2 * t + 1]()
-            nc.vector.tensor_tensor(trimmed[:, t, :], part[:], second, ALU.min)
+        scratch = [tile("scratch%d" % u, [P, 2, S], F32) for u in range(2)]
+
+        def differences(u):
+            for e in range(2):
+                nc.vector.tensor_tensor(scratch[u][:, e, :], members[u][:, e, 1:J:2], y_ps[2 * u + e][:], ALU.subtract)
+
+        def partial(u):
+            nc.vector.scalar_tensor_tensor(
+                scratch[1 - u][:], scratch[u][:], 0.0, members[u][:, :, 0:J:2], ALU.min, ALU.add
+            )
+
+        def trim(u):
+            nc.vector.tensor_tensor(trimmed[:, 2 * u : 2 * u + 2, :], scratch[1 - u][:], members[u][:, :, 1:J:2], ALU.min)
+
+        differences(0)
+        w2_q = quantize("w2", w2_grouped, N)
+        partial(0)
+        trim(0)
+        round_weight(w3_grouped, w3_raw, 0)
+        differences(1)
+        round_weight(w3_grouped, w3_raw, 1)
+        partial(1)
+        w3_q = quantize("w3", w3_grouped, N)
+        trim(1)
 
         at_n2 = [tile("at_n2_%d" % h, [P, PACK, HALF], F32) for h in range(2)]
         for h in range(2):
             for t in range(PACK):
                 nc.scalar.activation(at_n2[h][:, t, :], yg_win[t][:].indirect(n2_sb[:, 8 * h : 8 * h + 8]), ACT.Copy)
 
-        quantize_pair(w3_grouped, w3_q, 0)
+        rest = tile("rest", [P, PACK, S], F32)
+        larger = [scratch[0][:], trimmed[:, 0:2, :]]
+
+        def rest_of(t):
+            nc.vector.scalar_tensor_tensor(
+                rest[:, t, :], larger[t // 2][:, t % 2, :], gm_sb[:, t : t + 1], yg_win[t][:], ALU.mult, ALU.subtract
+            )
+
+        nc.vector.tensor_tensor(larger[0], at_n3[0][:], at_n4[0][:], ALU.max)
         z_grouped = tile("z_grouped", [P, S * PACK], BF16)
         nc.vector.tensor_tensor(
-            z_grouped[:].rearrange("p (c i t) -> p c t i", i=4, t=PACK),
-            weave(trimmed[:]),
+            woven(z_grouped),
+            by_fours(trimmed[:]),
             gn_sb[:].unsqueeze(1).unsqueeze(3).to_broadcast([P, S // 4, PACK, 4]),
             ALU.mult,
         )
-        quantize_pair(w3_grouped, w3_q, 1)
+        rest_of(0)
+        rest_of(1)
+        nc.vector.tensor_tensor(larger[1], at_n3[1][:], at_n4[1][:], ALU.max)
         z_q = quantize("z", z_grouped, S)
+        rest_of(2)
+        rest_of(3)
 
-        rest = tile("rest", [P, PACK, S], F32)
-        for step in range(PACK + 1):
-            if step < PACK:
-                nc.vector.tensor_tensor(trimmed[:, step, :], at_n3[step][:], at_n4[step][:], ALU.max)
-            if step > 0:
-                t = step - 1
-                nc.vector.scalar_tensor_tensor(
-                    rest[:, t, :], trimmed[:, t, :], gm_sb[:, t : t + 1], yg_win[t][:], ALU.mult, ALU.subtract
-                )
+        h_ps = [ps.tile([P, S], F32, name="h_ps%d" % t) for t in range(PACK)]
+        for t in range(PACK):
+            mx(h_ps[t][:], w2_q, slice(P * t, P * (t + 1)), z_q, slice(0, S), True, False)
 
-        h_ps = [
-            [ps.tile([P, HALF], F32, name="h_ps%d_%d" % (h, t), tag=("early%d", "late%d")[h] % t) for t in range(PACK)]
-            for h in range(2)
-        ]
-        everything = slice(0, P)
+        z2_q = (tile("z2_codes", [P, S], U32), tile("z2_scales", [P, S], U8))
         for h in range(2):
-            for t in range(PACK):
-                mx(h_ps[h][t][:], w2_q, slice(P * t, P * (t + 1)), z_q, slice(HALF * h, HALF * (h + 1)), True, False)
+            cols = slice(HALF * h, HALF * (h + 1))
+            z2_grouped = tile("z2_grouped%d" % h, [P, HALF * PACK], BF16)
+            nc.vector.tensor_tensor(woven(z2_grouped), by_fours(at_n2[h][:]), by_fours(rest[:, :, cols]), ALU.subtract)
+            nc.vector.quantize_mx(out=z2_q[0][:, cols].bitcast(FP8X4), scales=z2_q[1][:, cols], in_=z2_grouped[:])
+        for t in range(PACK):
+            mx(h_ps[t][:], w3_q, slice(P * t, P * (t + 1)), z2_q, slice(0, S), False, True)
 
-        z2_grouped = tile("z2_grouped", [P, HALF * PACK], BF16)
         h_win = [tile("h_win%d" % t, [P, H_WINDOW], F32) for t in range(PACK)]
-        for h in range(2):
-            nc.vector.tensor_tensor(
-                z2_grouped[:].rearrange("p (c i t) -> p c t i", i=4, t=PACK),
-                weave(at_n2[h][:]),
-                weave(rest[:, :, HALF * h : HALF * (h + 1)]),
-                ALU.subtract,
-            )
-            z2_q = quantize("z2_%d" % h, z2_grouped, HALF)
-            for t in range(PACK):
-                mx(h_ps[h][t][:], w3_q, slice(P * t, P * (t + 1)), z2_q, everything, False, True)
         for t in range(PACK):
-            nc.scalar.activation(h_win[t][:, 0:HALF], h_ps[0][t][:], ACT.Copy)
-        for t in range(PACK):
-            nc.vector.tensor_copy(h_win[t][:, HALF:S], h_ps[1][t][:])
+            nc.vector.tensor_copy(h_win[t][:, 0:S], h_ps[t][:])
 
         out_view = out.rearrange("(b t q) s -> t b q s", t=PACK, q=4)
-        for t in range(PACK):
-            gate = tile("gate%d" % t, [P, S], F32)
-            nc.scalar.activation(gate[:], h_win[t][:].indirect(n5_sb[:]), ACT.Sigmoid)
-            res = tile("res%d" % t, [P, S], F32)
-            nc.vector.tensor_tensor(res[:], h_win[t][:, 0:S], gate[:], ALU.mult)
-            nc.sync.dma_start(out_view[t], res[:])
+        pieces = [(t, 0, S) for t in range(PACK - 1)] + [(PACK - 1, 0, HALF), (PACK - 1, HALF, S)]
+        for t, lo, hi in pieces:
+            gate = tile("gate%d_%d" % (t, lo), [P, hi - lo], F32)
+            nc.scalar.activation(gate[:], h_win[t][:].indirect(n5_sb[:, lo // 16 : hi // 16]), ACT.Sigmoid)
+            res = tile("res%d_%d" % (t, lo), [P, hi - lo], F32)
+            nc.vector.tensor_tensor(res[:], h_win[t][:, lo:hi], gate[:], ALU.mult)
+            nc.sync.dma_start(out_view[t][:, :, lo:hi], res[:])

@@ -17,10 +17,12 @@ ACT = mybir.ActivationFunctionType
 
 P = 128
 PACK = 4
+RUN = 4
 HALF = S // 2
-Y_WINDOW = 1024
-H_WINDOW = 512
-SCALAR_Y = (0,)
+PAIR = 2 * P
+PER_COLUMN = 16
+Y_WINDOW = 2 * J
+H_WINDOW = 2 * S
 
 
 def tile_picked_joingpairtrimgate_none_p_kernel(
@@ -44,22 +46,34 @@ def tile_picked_joingpairtrimgate_none_p_kernel(
             nc.sync.dma_start(raw[:], src.rearrange("(p j) c -> p j c", j=PACK))
             return raw
 
-        def quantize(name, grouped, width):
-            codes = tile(name + "_codes", [P, width], U32)
-            scales = tile(name + "_scales", [P, width], U8)
-            nc.vector.quantize_mx(out=codes[:].bitcast(FP8X4), scales=scales[:], in_=grouped[:])
-            return codes, scales
+        def load_gain(name, src):
+            gain = tile(name, [P, PACK], F32)
+            nc.sync.dma_start(gain[:], src.rearrange("(p t) o -> p (t o)", t=PACK))
+            return gain
 
-        def mx(dst, lhs, lhs_cols, rhs, rhs_cols, start, stop):
+        def mx_operand(name, width):
+            return tile(name + "_codes", [P, width], U32), tile(name + "_scales", [P, width], U8)
+
+        def quantize(operand, cols, woven):
+            nc.vector.quantize_mx(out=operand[0][:, cols].bitcast(FP8X4), scales=operand[1][:, cols], in_=woven)
+
+        def multiply(dst, weights, t, moving, start, stop):
+            cols = slice(P * t, P * (t + 1))
             nc.tensor.matmul_mx(
                 out=dst,
-                lhsT=lhs[0][:, lhs_cols].bitcast(FP8X4),
-                lhsT_scale=lhs[1][:, lhs_cols],
-                rhs=rhs[0][:, rhs_cols].bitcast(FP8X4),
-                rhs_scale=rhs[1][:, rhs_cols],
+                lhsT=weights[0][:, cols].bitcast(FP8X4),
+                lhsT_scale=weights[1][:, cols],
+                rhs=moving[0][:].bitcast(FP8X4),
+                rhs_scale=moving[1][:],
                 start=start,
                 stop=stop,
             )
+
+        def look_up(dst, window, offsets, func):
+            nc.scalar.activation(dst, window[:].indirect(offsets), func)
+
+        def pair_cols(u):
+            return slice(PAIR * u, PAIR * (u + 1))
 
         scale_table = tile("scale_table", [P, T], U8)
         nc.gpsimd.memset(scale_table[:].bitcast(I32), 0)
@@ -78,78 +92,72 @@ def tile_picked_joingpairtrimgate_none_p_kernel(
         n1_sb = load_list("n1_sb", n1)
         n3_sb = load_list("n3_sb", n3)
         n4_sb = load_list("n4_sb", n4)
-        gn_sb = tile("gn_sb", [P, PACK], F32)
-        gm_sb = tile("gm_sb", [P, PACK], F32)
-        nc.sync.dma_start(gm_sb[:], gm.rearrange("(p t) o -> p (t o)", t=PACK))
-        w2_raw = [load_weight("w2_raw%d" % u, w2[:, u * N // 2 : (u + 1) * N // 2])[:] for u in range(2)]
+        gm_sb = load_gain("gm_sb", gm)
+        w2_raw = [load_weight("w2_raw%d" % u, w2[:, u * N // 2 : (u + 1) * N // 2]) for u in range(2)]
+        w3_raw = load_weight("w3_raw", w3)
         n2_sb = load_list("n2_sb", n2)
         n5_sb = load_list("n5_sb", n5)
-        w3_whole = load_weight("w3_raw", w3)
-        w3_raw = [w3_whole[:, :, u * N // 2 : (u + 1) * N // 2] for u in range(2)]
-        nc.sync.dma_start(gn_sb[:], gn.rearrange("(p t) o -> p (t o)", t=PACK))
+        gn_sb = load_gain("gn_sb", gn)
 
-        x_sc = tile("x_sc", [P, S], U8)
-        nc.vector.tensor_copy(x_sc[:], scale_table[:].indirect(offs_sb[:]))
+        x_mx = mx_operand("x", S)
+        nc.vector.tensor_copy(x_mx[1][:], scale_table[:].indirect(offs_sb[:]))
 
-        w1_q = []
-        w1_view = w1_raw[:].rearrange("p j (m t) -> p m t j", t=PACK)
-        w1_grouped = [tile("w1_grouped%d" % u, [P, 2 * P * PACK], BF16) for u in range(2)]
-        dsts = [g[:].rearrange("p (t m j) -> p m t j", t=2, j=PACK) for g in w1_grouped]
-        nc.vector.tensor_copy(dsts[0], w1_view[:, :, 0:2, :])
-        nc.scalar.activation(dsts[1], w1_view[:, :, 2:4, :], ACT.Copy)
+        w1_src = w1_raw[:].rearrange("p j (m t) -> p m t j", t=PACK)
+        w1_woven = [tile("w1_woven%d" % u, [P, PAIR * PACK], BF16) for u in range(2)]
+        w1_dst = [woven[:].rearrange("p (t m j) -> p m t j", t=2, j=PACK) for woven in w1_woven]
+        nc.vector.tensor_copy(w1_dst[0], w1_src[:, :, 0:2, :])
+        nc.scalar.activation(w1_dst[1], w1_src[:, :, 2:4, :], ACT.Copy)
+        w1_mx = [mx_operand("w1_%d" % u, PAIR) for u in range(2)]
         for u in range(2):
-            w1_q.append(quantize("w1_%d" % u, w1_grouped[u], 2 * P))
+            quantize(w1_mx[u], pair_cols(0), w1_woven[u][:])
 
-        x_cd = tile("x_cd", [P, S], U32)
-        nc.vector.tensor_copy(x_cd[:], word_table[:].bitcast(U32).indirect(offs_sb[:]))
-        x_q = (x_cd, x_sc)
+        nc.vector.tensor_copy(x_mx[0][:], word_table[:].indirect(offs_sb[:]))
 
         y_ps = [ps.tile([P, S], F32, name="y_ps%d" % t) for t in range(PACK)]
         for t in range(PACK):
-            mx(y_ps[t][:], w1_q[t // 2], slice(P * (t % 2), P * (t % 2 + 1)), x_q, slice(0, S), True, True)
+            multiply(y_ps[t][:], w1_mx[t // 2], t % 2, x_mx, True, True)
 
-        def round_weight(grouped, raw, u):
+        w2_woven = tile("w2_woven", [P, N * PACK], BF16)
+        w2_mx = mx_operand("w2", N)
+
+        def weave_w2(u):
             nc.vector.tensor_copy(
-                grouped[:].rearrange("p (t u b q j) -> p u t b j q", t=PACK, u=2, q=4, j=PACK)[:, u],
-                raw[u].rearrange("p j (b t q) -> p t b j q", t=PACK, q=4),
+                w2_woven[:].rearrange("p (t u b q j) -> p u t b j q", t=PACK, u=2, q=RUN, j=PACK)[:, u],
+                w2_raw[u][:].rearrange("p j (b t q) -> p t b j q", t=PACK, q=RUN),
             )
 
-        def woven(grouped):
-            return grouped[:].rearrange("p (c i t) -> p c t i", i=4, t=PACK)
+        def quantize_w2(u):
+            quantize(w2_mx, pair_cols(u), w2_woven[:, PAIR * PACK * u : PAIR * PACK * (u + 1)])
 
-        def by_fours(planes):
-            return planes.rearrange("p t (c i) -> p c t i", i=4)
-
-        w2_grouped = tile("w2_grouped", [P, N * PACK], BF16)
-        w3_grouped = tile("w3_grouped", [P, N * PACK], BF16)
-        round_weight(w2_grouped, w2_raw, 0)
+        weave_w2(0)
 
         y_win = [tile("y_win%d" % t, [P, Y_WINDOW], F32) for t in range(PACK)]
         members = [tile("members%d" % u, [P, 2, J], F32) for u in range(2)]
         for t in range(PACK):
-            if t in SCALAR_Y:
+            if t == 0:
                 nc.scalar.activation(y_win[t][:, 0:S], y_ps[t][:], ACT.Copy)
             else:
                 nc.vector.tensor_copy(y_win[t][:, 0:S], y_ps[t][:])
-            nc.scalar.activation(members[t // 2][:, t % 2, :], y_win[t][:].indirect(n1_sb[:]), ACT.Copy)
-        yg_win = [tile("yg_win%d" % t, [P, S], F32) for t in range(PACK)]
+            look_up(members[t // 2][:, t % 2, :], y_win[t], n1_sb[:], ACT.Copy)
+        gained_win = [tile("gained_win%d" % t, [P, S], F32) for t in range(PACK)]
+        for t in range(PACK):
+            nc.gpsimd.tensor_scalar(gained_win[t][:], y_win[t][:, 0:S], gm_sb[:, t : t + 1], 0.0, ALU.mult, ALU.add)
         at_n3 = [tile("at_n3_%d" % u, [P, 2, S], F32) for u in range(2)]
         at_n4 = [tile("at_n4_%d" % u, [P, 2, S], F32) for u in range(2)]
         for t in range(PACK):
-            nc.scalar.activation(at_n3[t // 2][:, t % 2, :], y_win[t][:].indirect(n3_sb[:]), ACT.Copy)
-            nc.scalar.activation(at_n4[t // 2][:, t % 2, :], y_win[t][:].indirect(n4_sb[:]), ACT.Copy)
-            nc.scalar.activation(yg_win[t][:], y_win[t][:, 0:S], ACT.Copy, scale=gm_sb[:, t : t + 1])
+            look_up(at_n3[t // 2][:, t % 2, :], y_win[t], n3_sb[:], ACT.Copy)
+            look_up(at_n4[t // 2][:, t % 2, :], y_win[t], n4_sb[:], ACT.Copy)
 
-        round_weight(w2_grouped, w2_raw, 1)
+        weave_w2(1)
 
         trimmed = tile("trimmed", [P, PACK, S], F32)
         scratch = [tile("scratch%d" % u, [P, 2, S], F32) for u in range(2)]
 
-        def differences(u):
-            for e in range(2):
-                nc.vector.tensor_tensor(scratch[u][:, e, :], members[u][:, e, 1:J:2], y_ps[2 * u + e][:], ALU.subtract)
+        def difference(t):
+            u, e = divmod(t, 2)
+            nc.vector.tensor_tensor(scratch[u][:, e, :], members[u][:, e, 1:J:2], y_ps[t][:], ALU.subtract)
 
-        def partial(u):
+        def add_first(u):
             nc.vector.scalar_tensor_tensor(
                 scratch[1 - u][:], scratch[u][:], 0.0, members[u][:, :, 0:J:2], ALU.min, ALU.add
             )
@@ -157,67 +165,100 @@ def tile_picked_joingpairtrimgate_none_p_kernel(
         def trim(u):
             nc.vector.tensor_tensor(trimmed[:, 2 * u : 2 * u + 2, :], scratch[1 - u][:], members[u][:, :, 1:J:2], ALU.min)
 
-        differences(0)
-        w2_q = quantize("w2", w2_grouped, N)
-        partial(0)
+        w3_woven = [tile("w3_woven%d" % u, [P, PAIR * PACK], BF16) for u in range(2)]
+        w3_mx = [mx_operand("w3_%d" % u, PAIR) for u in range(2)]
+
+        difference(0)
+        quantize_w2(0)
+        difference(1)
+        quantize_w2(1)
+        add_first(0)
         trim(0)
-        round_weight(w3_grouped, w3_raw, 0)
-        differences(1)
-        round_weight(w3_grouped, w3_raw, 1)
-        partial(1)
-        w3_q = quantize("w3", w3_grouped, N)
+        difference(2)
+        difference(3)
+        nc.vector.tensor_copy(
+            w3_woven[0][:].rearrange("p (t b q j) -> p t b j q", t=2, q=RUN, j=PACK),
+            w3_raw[:].rearrange("p j (b t q) -> p t b j q", t=PACK, q=RUN)[:, 0:2],
+        )
+        add_first(1)
+        quantize(w3_mx[0], pair_cols(0), w3_woven[0][:])
         trim(1)
 
-        at_n2 = [tile("at_n2_%d" % h, [P, PACK, HALF], F32) for h in range(2)]
-        for h in range(2):
-            for t in range(PACK):
-                nc.scalar.activation(at_n2[h][:, t, :], yg_win[t][:].indirect(n2_sb[:, 8 * h : 8 * h + 8]), ACT.Copy)
+        nc.scalar.copy(
+            w3_woven[1][:].rearrange("p (t b q j) -> p t b q j", t=2, q=RUN, j=PACK),
+            w3_raw[:].rearrange("p j (b t q) -> p t b q j", t=PACK, q=RUN)[:, 2:4],
+        )
 
-        rest = tile("rest", [P, PACK, S], F32)
+        at_n2 = [tile("at_n2_%d" % half, [P, PACK, HALF], F32) for half in range(2)]
+        list_cols = HALF // PER_COLUMN
+        for half in range(2):
+            for t in range(PACK):
+                offsets = n2_sb[:, list_cols * half : list_cols * (half + 1)]
+                look_up(at_n2[half][:, t, :], gained_win[t], offsets, ACT.Copy)
+
+        def woven_order(woven):
+            return woven[:].rearrange("p (c i t) -> p c t i", i=RUN, t=PACK)
+
+        def plane_order(planes):
+            return planes.rearrange("p t (c i) -> p c t i", i=RUN)
+
         larger = [scratch[0][:], trimmed[:, 0:2, :]]
+        minus_rest = tile("minus_rest", [P, PACK, S], F32)
+
+        def take_larger(u):
+            nc.vector.tensor_tensor(larger[u], at_n3[u][:], at_n4[u][:], ALU.max)
 
         def rest_of(t):
             nc.vector.scalar_tensor_tensor(
-                rest[:, t, :], larger[t // 2][:, t % 2, :], gm_sb[:, t : t + 1], yg_win[t][:], ALU.mult, ALU.subtract
+                minus_rest[:, t, :],
+                larger[t // 2][:, t % 2, :],
+                gm_sb[:, t : t + 1],
+                gained_win[t][:],
+                ALU.mult,
+                ALU.subtract,
             )
 
-        nc.vector.tensor_tensor(larger[0], at_n3[0][:], at_n4[0][:], ALU.max)
-        z_grouped = tile("z_grouped", [P, S * PACK], BF16)
+        take_larger(0)
+        z_woven = tile("z_woven", [P, S * PACK], BF16)
         nc.vector.tensor_tensor(
-            woven(z_grouped),
-            by_fours(trimmed[:]),
-            gn_sb[:].unsqueeze(1).unsqueeze(3).to_broadcast([P, S // 4, PACK, 4]),
+            woven_order(z_woven),
+            plane_order(trimmed[:]),
+            gn_sb[:].unsqueeze(1).unsqueeze(3).to_broadcast([P, S // RUN, PACK, RUN]),
             ALU.mult,
         )
         rest_of(0)
         rest_of(1)
-        nc.vector.tensor_tensor(larger[1], at_n3[1][:], at_n4[1][:], ALU.max)
-        z_q = quantize("z", z_grouped, S)
+        take_larger(1)
+        z_mx = mx_operand("z", S)
+        quantize(z_mx, slice(0, S), z_woven[:])
         rest_of(2)
         rest_of(3)
+        quantize(w3_mx[1], pair_cols(0), w3_woven[1][:])
 
         h_ps = [ps.tile([P, S], F32, name="h_ps%d" % t) for t in range(PACK)]
         for t in range(PACK):
-            mx(h_ps[t][:], w2_q, slice(P * t, P * (t + 1)), z_q, slice(0, S), True, False)
+            multiply(h_ps[t][:], w2_mx, t, z_mx, True, False)
 
-        z2_q = (tile("z2_codes", [P, S], U32), tile("z2_scales", [P, S], U8))
-        for h in range(2):
-            cols = slice(HALF * h, HALF * (h + 1))
-            z2_grouped = tile("z2_grouped%d" % h, [P, HALF * PACK], BF16)
-            nc.vector.tensor_tensor(woven(z2_grouped), by_fours(at_n2[h][:]), by_fours(rest[:, :, cols]), ALU.subtract)
-            nc.vector.quantize_mx(out=z2_q[0][:, cols].bitcast(FP8X4), scales=z2_q[1][:, cols], in_=z2_grouped[:])
+        z2_mx = mx_operand("z2", S)
+        for half in range(2):
+            cols = slice(HALF * half, HALF * (half + 1))
+            z2_woven = tile("z2_woven%d" % half, [P, HALF * PACK], BF16)
+            nc.vector.tensor_tensor(
+                woven_order(z2_woven), plane_order(at_n2[half][:]), plane_order(minus_rest[:, :, cols]), ALU.subtract
+            )
+            quantize(z2_mx, cols, z2_woven[:])
         for t in range(PACK):
-            mx(h_ps[t][:], w3_q, slice(P * t, P * (t + 1)), z2_q, slice(0, S), False, True)
+            multiply(h_ps[t][:], w3_mx[t // 2], t % 2, z2_mx, False, True)
 
         h_win = [tile("h_win%d" % t, [P, H_WINDOW], F32) for t in range(PACK)]
         for t in range(PACK):
             nc.vector.tensor_copy(h_win[t][:, 0:S], h_ps[t][:])
 
-        out_view = out.rearrange("(b t q) s -> t b q s", t=PACK, q=4)
+        out_planes = out.rearrange("(b t q) s -> t b q s", t=PACK, q=RUN)
         pieces = [(t, 0, S) for t in range(PACK - 1)] + [(PACK - 1, 0, HALF), (PACK - 1, HALF, S)]
         for t, lo, hi in pieces:
             gate = tile("gate%d_%d" % (t, lo), [P, hi - lo], F32)
-            nc.scalar.activation(gate[:], h_win[t][:].indirect(n5_sb[:, lo // 16 : hi // 16]), ACT.Sigmoid)
-            res = tile("res%d_%d" % (t, lo), [P, hi - lo], F32)
-            nc.vector.tensor_tensor(res[:], h_win[t][:, lo:hi], gate[:], ALU.mult)
-            nc.sync.dma_start(out_view[t][:, :, lo:hi], res[:])
+            look_up(gate[:], h_win[t], n5_sb[:, lo // PER_COLUMN : hi // PER_COLUMN], ACT.Sigmoid)
+            gated = tile("gated%d_%d" % (t, lo), [P, hi - lo], F32)
+            nc.vector.tensor_tensor(gated[:], h_win[t][:, lo:hi], gate[:], ALU.mult)
+            nc.sync.dma_start(out_planes[t][:, :, lo:hi], gated[:])

from contextlib import ExitStack

import concourse.mybir as mybir

K, T, S, N, H, J = 512, 2048, 256, 512, 512, 512
FLOPS = 2 * S * (K * H + 2 * H * N)

F32 = mybir.dt.float32
BF16 = mybir.dt.bfloat16
I32 = mybir.dt.int32
U32 = mybir.dt.uint32
U16 = mybir.dt.uint16
U8 = mybir.dt.uint8
FP8X4 = mybir.dt.float8_e4m3fn_x4
ALU = mybir.AluOpType
ACT = mybir.ActivationFunctionType

P = 128
PACK = 4
RUN = 4
HALF = S // 2
PAIR = 2 * P
PER_COLUMN = 16
Y_WINDOW = 2 * J
H_WINDOW = 2 * S


def tile_picked_joingpairtrimgate_none_p_kernel(
    tc, x_words, x_scales, w1, gn, gm, w2, w3, offs, n1, n2, n3, n4, n5, out
):
    nc = tc.nc
    with ExitStack() as ctx:
        sb = ctx.enter_context(tc.tile_pool(name="sb", bufs=1))
        ps = ctx.enter_context(tc.psum_pool(name="ps", bufs=1))

        def tile(name, shape, dtype):
            return sb.tile(shape, dtype, name=name, align_bytes=64)

        def load_list(name, src):
            lst = tile(name, list(src.shape), U16)
            nc.sync.dma_start(lst[:], src)
            return lst

        def load_weight(name, src):
            raw = tile(name, [P, PACK, src.shape[1]], F32)
            nc.sync.dma_start(raw[:], src.rearrange("(p j) c -> p j c", j=PACK))
            return raw

        def load_gain(name, src):
            gain = tile(name, [P, PACK], F32)
            nc.sync.dma_start(gain[:], src.rearrange("(p t) o -> p (t o)", t=PACK))
            return gain

        def mx_operand(name, width):
            return tile(name + "_codes", [P, width], U32), tile(name + "_scales", [P, width], U8)

        def quantize(operand, cols, woven):
            nc.vector.quantize_mx(out=operand[0][:, cols].bitcast(FP8X4), scales=operand[1][:, cols], in_=woven)

        def multiply(dst, weights, t, moving, start, stop):
            cols = slice(P * t, P * (t + 1))
            nc.tensor.matmul_mx(
                out=dst,
                lhsT=weights[0][:, cols].bitcast(FP8X4),
                lhsT_scale=weights[1][:, cols],
                rhs=moving[0][:].bitcast(FP8X4),
                rhs_scale=moving[1][:],
                start=start,
                stop=stop,
            )

        def look_up(dst, window, offsets, func):
            nc.scalar.activation(dst, window[:].indirect(offsets), func)

        def pair_cols(u):
            return slice(PAIR * u, PAIR * (u + 1))

        scale_table = tile("scale_table", [P, T], U8)
        nc.gpsimd.memset(scale_table[:].bitcast(I32), 0)
        warm = tile("warm", [P, 2], F32)
        nc.vector.memset(warm[:, 0:1], 0.0)
        nc.scalar.activation(warm[:, 1:2], warm[:, 0:1], ACT.Sigmoid)
        w1_raw = load_weight("w1_raw", w1)
        offs_sb = load_list("offs_sb", offs)
        for quad in range(4):
            nc.sync.dma_start(
                scale_table[32 * quad : 32 * quad + 4, :].bitcast(I32),
                x_scales[0, 4 * quad : 4 * quad + 4, :].bitcast(I32),
            )
        word_table = tile("word_table", [P, T], U32)
        nc.sync.dma_start(word_table[:].bitcast(I32), x_words[0].rearrange("p n t -> p (n t)").bitcast(I32))
        n1_sb = load_list("n1_sb", n1)
        n3_sb = load_list("n3_sb", n3)
        n4_sb = load_list("n4_sb", n4)
        gm_sb = load_gain("gm_sb", gm)
        w2_raw = [load_weight("w2_raw%d" % u, w2[:, u * N // 2 : (u + 1) * N // 2]) for u in range(2)]
        w3_raw = load_weight("w3_raw", w3)
        n2_sb = load_list("n2_sb", n2)
        n5_sb = load_list("n5_sb", n5)
        gn_sb = load_gain("gn_sb", gn)

        x_mx = mx_operand("x", S)
        nc.vector.tensor_copy(x_mx[1][:], scale_table[:].indirect(offs_sb[:]))

        w1_src = w1_raw[:].rearrange("p j (m t) -> p m t j", t=PACK)
        w1_woven = [tile("w1_woven%d" % u, [P, PAIR * PACK], BF16) for u in range(2)]
        w1_dst = [woven[:].rearrange("p (t m j) -> p m t j", t=2, j=PACK) for woven in w1_woven]
        nc.vector.tensor_copy(w1_dst[0], w1_src[:, :, 0:2, :])
        nc.scalar.activation(w1_dst[1], w1_src[:, :, 2:4, :], ACT.Copy)
        w1_mx = [mx_operand("w1_%d" % u, PAIR) for u in range(2)]
        for u in range(2):
            quantize(w1_mx[u], pair_cols(0), w1_woven[u][:])

        nc.vector.tensor_copy(x_mx[0][:], word_table[:].indirect(offs_sb[:]))

        y_ps = [ps.tile([P, S], F32, name="y_ps%d" % t) for t in range(PACK)]
        for t in range(PACK):
            multiply(y_ps[t][:], w1_mx[t // 2], t % 2, x_mx, True, True)

        w2_woven = tile("w2_woven", [P, N * PACK], BF16)
        w2_mx = mx_operand("w2", N)

        def weave_w2(u):
            nc.vector.tensor_copy(
                w2_woven[:].rearrange("p (t u b q j) -> p u t b j q", t=PACK, u=2, q=RUN, j=PACK)[:, u],
                w2_raw[u][:].rearrange("p j (b t q) -> p t b j q", t=PACK, q=RUN),
            )

        def quantize_w2(u):
            quantize(w2_mx, pair_cols(u), w2_woven[:, PAIR * PACK * u : PAIR * PACK * (u + 1)])

        weave_w2(0)

        y_win = [tile("y_win%d" % t, [P, Y_WINDOW], F32) for t in range(PACK)]
        members = [tile("members%d" % u, [P, 2, J], F32) for u in range(2)]
        for t in range(PACK):
            if t == 0:
                nc.scalar.activation(y_win[t][:, 0:S], y_ps[t][:], ACT.Copy)
            else:
                nc.vector.tensor_copy(y_win[t][:, 0:S], y_ps[t][:])
            look_up(members[t // 2][:, t % 2, :], y_win[t], n1_sb[:], ACT.Copy)
        gained_win = [tile("gained_win%d" % t, [P, S], F32) for t in range(PACK)]
        for t in range(PACK):
            nc.gpsimd.tensor_scalar(gained_win[t][:], y_win[t][:, 0:S], gm_sb[:, t : t + 1], 0.0, ALU.mult, ALU.add)
        at_n3 = [tile("at_n3_%d" % u, [P, 2, S], F32) for u in range(2)]
        at_n4 = [tile("at_n4_%d" % u, [P, 2, S], F32) for u in range(2)]
        for t in range(PACK):
            look_up(at_n3[t // 2][:, t % 2, :], y_win[t], n3_sb[:], ACT.Copy)
            look_up(at_n4[t // 2][:, t % 2, :], y_win[t], n4_sb[:], ACT.Copy)

        weave_w2(1)

        trimmed = tile("trimmed", [P, PACK, S], F32)
        scratch = [tile("scratch%d" % u, [P, 2, S], F32) for u in range(2)]

        def difference(t):
            u, e = divmod(t, 2)
            nc.vector.tensor_tensor(scratch[u][:, e, :], members[u][:, e, 1:J:2], y_ps[t][:], ALU.subtract)

        def add_first(u):
            nc.vector.scalar_tensor_tensor(
                scratch[1 - u][:], scratch[u][:], 0.0, members[u][:, :, 0:J:2], ALU.min, ALU.add
            )

        def trim(u):
            nc.vector.tensor_tensor(trimmed[:, 2 * u : 2 * u + 2, :], scratch[1 - u][:], members[u][:, :, 1:J:2], ALU.min)

        w3_woven = [tile("w3_woven%d" % u, [P, PAIR * PACK], BF16) for u in range(2)]
        w3_mx = [mx_operand("w3_%d" % u, PAIR) for u in range(2)]

        difference(0)
        quantize_w2(0)
        difference(1)
        quantize_w2(1)
        add_first(0)
        trim(0)
        difference(2)
        difference(3)
        nc.vector.tensor_copy(
            w3_woven[0][:].rearrange("p (t b q j) -> p t b j q", t=2, q=RUN, j=PACK),
            w3_raw[:].rearrange("p j (b t q) -> p t b j q", t=PACK, q=RUN)[:, 0:2],
        )
        add_first(1)
        quantize(w3_mx[0], pair_cols(0), w3_woven[0][:])
        trim(1)

        nc.scalar.copy(
            w3_woven[1][:].rearrange("p (t b q j) -> p t b q j", t=2, q=RUN, j=PACK),
            w3_raw[:].rearrange("p j (b t q) -> p t b q j", t=PACK, q=RUN)[:, 2:4],
        )

        at_n2 = [tile("at_n2_%d" % half, [P, PACK, HALF], F32) for half in range(2)]
        list_cols = HALF // PER_COLUMN
        for half in range(2):
            for t in range(PACK):
                offsets = n2_sb[:, list_cols * half : list_cols * (half + 1)]
                look_up(at_n2[half][:, t, :], gained_win[t], offsets, ACT.Copy)

        def woven_order(woven):
            return woven[:].rearrange("p (c i t) -> p c t i", i=RUN, t=PACK)

        def plane_order(planes):
            return planes.rearrange("p t (c i) -> p c t i", i=RUN)

        larger = [scratch[0][:], trimmed[:, 0:2, :]]
        minus_rest = tile("minus_rest", [P, PACK, S], F32)

        def take_larger(u):
            nc.vector.tensor_tensor(larger[u], at_n3[u][:], at_n4[u][:], ALU.max)

        def rest_of(t):
            nc.vector.scalar_tensor_tensor(
                minus_rest[:, t, :],
                larger[t // 2][:, t % 2, :],
                gm_sb[:, t : t + 1],
                gained_win[t][:],
                ALU.mult,
                ALU.subtract,
            )

        take_larger(0)
        z_woven = tile("z_woven", [P, S * PACK], BF16)
        nc.vector.tensor_tensor(
            woven_order(z_woven),
            plane_order(trimmed[:]),
            gn_sb[:].unsqueeze(1).unsqueeze(3).to_broadcast([P, S // RUN, PACK, RUN]),
            ALU.mult,
        )
        rest_of(0)
        rest_of(1)
        take_larger(1)
        z_mx = mx_operand("z", S)
        quantize(z_mx, slice(0, S), z_woven[:])
        rest_of(2)
        rest_of(3)
        quantize(w3_mx[1], pair_cols(0), w3_woven[1][:])

        h_ps = [ps.tile([P, S], F32, name="h_ps%d" % t) for t in range(PACK)]
        for t in range(PACK):
            multiply(h_ps[t][:], w2_mx, t, z_mx, True, False)

        z2_mx = mx_operand("z2", S)
        for half in range(2):
            cols = slice(HALF * half, HALF * (half + 1))
            z2_woven = tile("z2_woven%d" % half, [P, HALF * PACK], BF16)
            nc.vector.tensor_tensor(
                woven_order(z2_woven), plane_order(at_n2[half][:]), plane_order(minus_rest[:, :, cols]), ALU.subtract
            )
            quantize(z2_mx, cols, z2_woven[:])
        for t in range(PACK):
            multiply(h_ps[t][:], w3_mx[t // 2], t % 2, z2_mx, False, True)

        h_win = [tile("h_win%d" % t, [P, H_WINDOW], F32) for t in range(PACK)]
        for t in range(PACK):
            nc.vector.tensor_copy(h_win[t][:, 0:S], h_ps[t][:])

        out_planes = out.rearrange("(b t q) s -> t b q s", t=PACK, q=RUN)
        pieces = [(t, 0, S) for t in range(PACK - 1)] + [(PACK - 1, 0, HALF), (PACK - 1, HALF, S)]
        for t, lo, hi in pieces:
            gate = tile("gate%d_%d" % (t, lo), [P, hi - lo], F32)
            look_up(gate[:], h_win[t], n5_sb[:, lo // PER_COLUMN : hi // PER_COLUMN], ACT.Sigmoid)
            gated = tile("gated%d_%d" % (t, lo), [P, hi - lo], F32)
            nc.vector.tensor_tensor(gated[:], h_win[t][:, lo:hi], gate[:], ALU.mult)
            nc.sync.dma_start(out_planes[t][:, :, lo:hi], gated[:])
